import numpy as np
import ml_dtypes


def mxq(x, axis, fmt="e4m3"):
    dtype, down = {"e4m3": (ml_dtypes.float8_e4m3fn, 7), "e5m2": (ml_dtypes.float8_e5m2, 14)}[fmt]
    v = np.moveaxis(np.asarray(x, np.float32).astype(ml_dtypes.bfloat16).astype(np.float64), axis, -1)
    blocks = v.reshape(v.shape[:-1] + (-1, 32))
    amax = np.abs(blocks).max(-1, keepdims=True)
    byte = np.maximum(np.where(amax > 0, np.frexp(amax)[1] - 1 + 127, 0) - down, 1)
    scale = np.exp2(byte - 127.0)
    codes = (blocks / scale).astype(np.float32).astype(dtype).astype(np.float64)
    return np.moveaxis((codes * scale).reshape(v.shape), -1, axis)


WIDE = False


def mx_kscale(k):
    if not WIDE:
        return np.ones(k)
    levels = np.array([10, -10, 5, -5, 0])
    if k % 512:
        return np.exp2(np.random.permutation(np.resize(levels, k // 32))).repeat(32)
    a = np.empty((k // 512, 16))
    for p in range(k // 512):
        a[p, :8] = np.random.permutation(np.resize(levels, 8))
        for g in range(8):
            far = levels[np.abs(levels - a[p, g]) >= 10]
            a[p, g + 8] = far[np.random.randint(len(far))]
    return np.exp2(a.ravel()).repeat(32)


def f64(x):
    return np.asarray(x).astype(np.float64)


def striped(idx):
    return np.tile(idx.reshape(-1, 16).T, (8, 1)).astype(np.uint16)


def unstriped(offs):
    return offs[:16].T.reshape(-1).astype(np.int64)


def pack_weight(w):
    k, n = w.shape
    w = f64(np.asarray(w, np.float32).astype(ml_dtypes.bfloat16)).reshape(k // 32, 32, n)
    amax = np.abs(w).max(1)
    byte = np.clip(np.where(amax > 0, np.frexp(amax)[1] - 1 + 127 - 7, 1), 1, 254)
    scaled = (w * np.exp2(127.0 - byte)[:, None, :]).reshape(k, n).astype(np.float32)
    words = np.ascontiguousarray(scaled.reshape(k // 512, 128, 4, n).transpose(0, 1, 3, 2)).astype(ml_dtypes.float8_e4m3fn).view(np.uint8)
    return words, np.ascontiguousarray(byte.astype(np.uint8).reshape(k // 512, 16, n))


def unpack_weight(words, scales):
    g, p, n, _ = words.shape
    vals = np.ascontiguousarray(words).view(ml_dtypes.float8_e4m3fn).astype(np.float64) * np.repeat(np.exp2(scales.astype(np.float64) - 127.0), 8, axis=1)[..., None]
    return vals.transpose(0, 1, 3, 2).reshape(g * 512, n)


def sigmoid(v):
    return 1.0 / (1.0 + np.exp(-np.maximum(v, -700.0)))


K, T, S, N, D = 512, 2048, 512, 128, 3
P = 2 ** 7


def setup_inputs():
    n = np.random.standard_normal
    s = mx_kscale(K)[:, None]
    packed_xT = pack_weight(n((K, T)) * s)
    return {
        "x_words": packed_xT[0],
        "x_scales": packed_xT[1],
        "w1": (n((K, N)) / np.sqrt(K) / s).astype(np.float32),
        "gain": (np.tile(np.random.uniform(0.05, 0.6, (D, 1, S)), (1, P, 1))).astype(np.float32),
        "hh": (np.tile(np.random.uniform(0.6, 1.6, S), (P, 1))).astype(np.float32),
        "noise": (np.random.uniform(0.05, 0.4, (N, 1))).astype(np.float32),
        "pri": (np.tile(np.random.uniform(0.5, 1.5, S), (P, 1))).astype(np.float32),
        "offs": striped(np.random.permutation(T)[:S]),
        "pos1": striped(np.random.permutation(S)[:S]),
        "pos2": striped(np.random.permutation(S)[:S]),
        "pos3": striped(np.random.permutation(S)[:S]),
    }


def reference(x_words, x_scales, w1, gain, hh, noise, pri, offs, pos1, pos2, pos3):
    xq = unpack_weight(x_words, x_scales)[:, unstriped(offs)]
    y = mxq(f64(w1), 0, "e4m3").T @ xq
    pp = sigmoid(y)
    bf = np.sqrt(pp)
    den = ((f64(hh)[:1]) ** 2) * pp + pp[:, unstriped(pos1)] * f64(gain)[0, :1] + pp[:, unstriped(pos2)] * f64(gain)[1, :1] + pp[:, unstriped(pos3)] * f64(gain)[2, :1] + f64(noise)
    ru = (f64(hh)[:1] * bf) / den
    return f64(pri)[:1] / (-1.0 * ((ru * f64(hh)[:1]) * bf) + 1.0)

@@ -1,0 +1,139 @@
+from contextlib import ExitStack
+
+import concourse.mybir as mybir
+from concourse.masks import make_identity
+
+K, T, S, M, D = 512, 2048, 512, 128, 3
+P = 128
+PACK = 4
+FLOPS = 2 * K * M * S
+
+F32 = mybir.dt.float32
+BF16 = mybir.dt.bfloat16
+I32 = mybir.dt.int32
+U32 = mybir.dt.uint32
+U16 = mybir.dt.uint16
+U8 = mybir.dt.uint8
+FP8X4 = mybir.dt.float8_e4m3fn_x4
+ALU = mybir.AluOpType
+ACT = mybir.ActivationFunctionType
+
+HALF = S // 2
+BLK = 128
+CHUNKS = ((0, 256), (256, 128), (384, 128))
+
+
+def tile_picked_ywmmse_wgt_p_kernel(tc, x_words, x_scales, w1, gain, hh, noise, pri, offs, pos1, pos2, pos3, out):
+    nc = tc.nc
+    with ExitStack() as ctx:
+        keep = ctx.enter_context(tc.tile_pool(name="keep", bufs=1))
+        psum = ctx.enter_context(tc.psum_pool(name="psum", bufs=1))
+
+        scales = keep.tile([P, T], U8, name="scales")
+        nc.vector.memset(scales[:, : T // 2].bitcast(I32), 0)
+        nc.gpsimd.memset(scales[:, T // 2 :].bitcast(I32), 0)
+        warm = keep.tile([P, 2], F32, name="warm")
+        nc.vector.memset(warm[:, 0:1], 0.0)
+        warm_o = keep.tile([P, 2], F32, name="warm_o")
+        nc.scalar.activation(warm_o[:, 0:1], warm[:, 0:1], ACT.Sigmoid)
+
+        pos_t = [keep.tile([P, S // 16], U16, name="pos_t%d" % d) for d in range(D)]
+        offs_t = keep.tile([P, S // 16], U16, name="offs_t")
+        nc.sync.dma_start(offs_t[:], offs)
+        w_raw = keep.tile([P, PACK, M], F32, name="w_raw")
+        nc.sync.dma_start(w_raw[:], w1.rearrange("(p j) m -> p j m", j=PACK))
+        noise_t = keep.tile([P, 1], F32, name="noise_t")
+        nc.sync.dma_start(noise_t[:], noise)
+        for q in range(4):
+            nc.sync.dma_start(scales[32 * q : 32 * q + 4, :].bitcast(I32), x_scales[0, 4 * q : 4 * q + 4, :].bitcast(I32))
+        words = keep.tile([P, T], I32, name="words")
+        nc.sync.dma_start(words[:], x_words[0].rearrange("p n t -> p (n t)").bitcast(I32))
+
+        rows = keep.tile([P, BLK], F32, name="rows")
+        nc.gpsimd.memset(rows[:], 0.0)
+        ident = keep.tile([P, P], F32, name="ident")
+        make_identity(nc, ident[:])
+        for t, pos in zip(pos_t, (pos1, pos2, pos3)):
+            nc.sync.dma_start(t[:], pos)
+        gains = []
+        for h in range(2):
+            t = keep.tile([P, D, HALF], F32, name="gain%d" % h)
+            nc.sync.dma_start(t[:], gain[:, :, h * HALF : (h + 1) * HALF].rearrange("d p s -> p d s"))
+            gains.append(t)
+            if h == 0:
+                nc.sync.dma_start(rows[0:4, :], hh[0, :].rearrange("(b i) -> b i", i=BLK))
+                nc.sync.dma_start(rows[4:8, :], pri[0, :].rearrange("(b i) -> b i", i=BLK))
+
+        w_bf = keep.tile([P, M, PACK], BF16, name="w_bf", align_bytes=64)
+        nc.scalar.copy(w_bf[:], w_raw[:].rearrange("p j m -> p m j"))
+        w_codes = keep.tile([P, M], U32, name="w_codes", align_bytes=64)
+        w_scales = keep.tile([P, M], U8, name="w_scales", align_bytes=64)
+        nc.vector.quantize_mx(out=w_codes[:].bitcast(FP8X4), scales=w_scales[:], in_=w_bf[:].rearrange("p m j -> p (m j)"))
+
+
+        def turn(dst, src, start, stop):
+            nc.tensor.matmul(dst, lhsT=src, rhs=ident[:], is_transpose=True, start=start, stop=stop)
+
+        sums = []
+        for c, (c0, w) in enumerate(CHUNKS):
+            acc = psum.tile([P, w], F32, name="acc%d" % c)
+            for b in range(w // BLK):
+                turn(acc[:, b * BLK : (b + 1) * BLK], noise_t[:, 0:1].to_broadcast([P, BLK]), b == 0, False)
+            sums.append(acc)
+
+        xs = []
+        for h in range(2):
+            t = keep.tile([P, HALF], U8, name="xs%d" % h, align_bytes=64)
+            nc.vector.tensor_copy(t[:], scales[:].indirect(offs_t[:, h * 16 : (h + 1) * 16]))
+            xs.append(t)
+        pp = keep.tile([P, S], F32, name="pp")
+        for h in range(2):
+            xw = keep.tile([P, HALF], U32, name="xw%d" % h, align_bytes=64)
+            nc.vector.tensor_copy(xw[:], words[:].bitcast(U32).indirect(offs_t[:, h * 16 : (h + 1) * 16]))
+            bank = psum.tile([P, S], F32, name="y%d" % h, tag="y%d" % h)
+            y = bank[:, :HALF]
+            nc.tensor.matmul_mx(out=y, lhsT=w_codes[:].bitcast(FP8X4), lhsT_scale=w_scales[:],
+                                rhs=xw[:].bitcast(FP8X4), rhs_scale=xs[h][:], start=True, stop=True)
+            nc.scalar.activation(pp[:, h * HALF : (h + 1) * HALF], y, ACT.Sigmoid)
+        nc.tensor.transpose(bank[:, HALF : HALF + BLK], rows[:], ident[:])
+        cols_t = keep.tile([P, 8], F32, name="cols_t")
+        nc.scalar.copy(cols_t[:], bank[:, HALF : HALF + 8])
+        nc.scalar.activation(warm_o[:, 1:2], pp[:, S - 1 : S], ACT.Abs_reciprocal_sqrt)
+
+        pp_T = psum.tile([P, S], F32, name="pp_T", tag="turn")
+        for b in range(S // BLK):
+            nc.tensor.transpose(pp_T[:, b * BLK : (b + 1) * BLK], pp[:, b * BLK : (b + 1) * BLK], ident[:])
+        res = []
+        for c, (c0, w) in enumerate(CHUNKS):
+            acc = psum.tile([P, w], F32, name="res%d" % c, tag="y0" if c == 0 else "res%d" % c)
+            for b in range(w // BLK):
+                g = c0 // BLK + b
+                turn(acc[:, b * BLK : (b + 1) * BLK], cols_t[:, 4 + g : 5 + g].to_broadcast([P, BLK]), b == 0, False)
+            res.append(acc)
+
+        rs = []
+        for c, (c0, w) in enumerate(CHUNKS):
+            nb = w // BLK
+            for d in range(D):
+                t = keep.tile([P, w], F32, name="t%d_%d" % (c, d))
+                nc.vector.tensor_tensor(t[:], pp[:].indirect(pos_t[d][:, c0 // 16 : (c0 + w) // 16]), gains[c0 // HALF][:, d, c0 % HALF : c0 % HALF + w], ALU.mult)
+                for b in range(nb):
+                    turn(sums[c][:, b * BLK : (b + 1) * BLK], t[:, b * BLK : (b + 1) * BLK], False, d == D - 1 and b == nb - 1)
+            s = keep.tile([P, w], F32, name="s%d" % c)
+            nc.scalar.activation(s[:], sums[c][:], ACT.Abs_reciprocal_sqrt)
+            r = keep.tile([P, w], F32, name="r%d" % c)
+            for b in range(nb):
+                g = c0 // BLK + b
+                nc.scalar.activation(r[:, b * BLK : (b + 1) * BLK], s[:, b * BLK : (b + 1) * BLK], ACT.Square, scale=cols_t[:, g : g + 1])
+            rs.append(r)
+        for c, (c0, w) in enumerate(CHUNKS):
+            nb = w // BLK
+            x = keep.tile([P, w], F32, name="x%d" % c)
+            for b in range(nb):
+                g = c0 // BLK + b
+                blk = slice(b * BLK, (b + 1) * BLK)
+                nc.vector.scalar_tensor_tensor(x[:, blk], rs[c][:, blk], cols_t[:, 4 + g : 5 + g], pp_T[:, g * BLK : (g + 1) * BLK], ALU.mult, ALU.mult)
+                turn(res[c][:, blk], x[:, blk], False, b == nb - 1)
+            o = keep.tile([P, w], F32, name="o%d" % c)
+            nc.vector.tensor_copy(o[:], res[c][:])
+            nc.sync.dma_start(out[:, c0 : c0 + w], o[:])

@@ -20,7 +20,9 @@ ACT = mybir.ActivationFunctionType
 
 HALF = S // 2
 BLK = 128
-CHUNKS = ((0, 256), (256, 128), (384, 128))
+TURNED = ((0, 256), (256, 128))
+LAST = S - BLK
+EARLY = 512
 
 
 def tile_picked_ywmmse_wgt_p_kernel(tc, x_words, x_scales, w1, gain, hh, noise, pri, offs, pos1, pos2, pos3, out):
@@ -38,31 +40,33 @@ def tile_picked_ywmmse_wgt_p_kernel(tc, x_words, x_scales, w1, gain, hh, noise, 
         nc.scalar.activation(warm_o[:, 0:1], warm[:, 0:1], ACT.Sigmoid)
 
         pos_t = [keep.tile([P, S // 16], U16, name="pos_t%d" % d) for d in range(D)]
-        offs_t = keep.tile([P, S // 16], U16, name="offs_t")
-        nc.sync.dma_start(offs_t[:], offs)
         w_raw = keep.tile([P, PACK, M], F32, name="w_raw")
         nc.sync.dma_start(w_raw[:], w1.rearrange("(p j) m -> p j m", j=PACK))
-        noise_t = keep.tile([P, 1], F32, name="noise_t")
-        nc.sync.dma_start(noise_t[:], noise)
+        words = keep.tile([P, T], I32, name="words")
+        words_hbm = x_words[0].rearrange("p n t -> p (n t)").bitcast(I32)
+        nc.sync.dma_start(words[:, :EARLY], words_hbm[:, :EARLY])
+        offs_t = keep.tile([P, S // 16], U16, name="offs_t")
+        nc.sync.dma_start(offs_t[:], offs)
         for q in range(4):
             nc.sync.dma_start(scales[32 * q : 32 * q + 4, :].bitcast(I32), x_scales[0, 4 * q : 4 * q + 4, :].bitcast(I32))
-        words = keep.tile([P, T], I32, name="words")
-        nc.sync.dma_start(words[:], x_words[0].rearrange("p n t -> p (n t)").bitcast(I32))
+        nc.sync.dma_start(words[:, EARLY:], words_hbm[:, EARLY:])
 
         rows = keep.tile([P, BLK], F32, name="rows")
         nc.gpsimd.memset(rows[:], 0.0)
         ident = keep.tile([P, P], F32, name="ident")
         make_identity(nc, ident[:])
+        nc.sync.dma_start(rows[0:4, :], hh[0, :].rearrange("(b i) -> b i", i=BLK))
+        nc.sync.dma_start(rows[4:8, :], pri[0, :].rearrange("(b i) -> b i", i=BLK))
         for t, pos in zip(pos_t, (pos1, pos2, pos3)):
             nc.sync.dma_start(t[:], pos)
+        noise_t = keep.tile([P, 1], F32, name="noise_t")
         gains = []
         for h in range(2):
-            t = keep.tile([P, D, HALF], F32, name="gain%d" % h)
+            t = keep.tile([P, D, HALF], F32, name="gain%d" % h, tag="gain%d" % h)
             nc.sync.dma_start(t[:], gain[:, :, h * HALF : (h + 1) * HALF].rearrange("d p s -> p d s"))
             gains.append(t)
             if h == 0:
-                nc.sync.dma_start(rows[0:4, :], hh[0, :].rearrange("(b i) -> b i", i=BLK))
-                nc.sync.dma_start(rows[4:8, :], pri[0, :].rearrange("(b i) -> b i", i=BLK))
+                nc.sync.dma_start(noise_t[:], noise)
 
         w_bf = keep.tile([P, M, PACK], BF16, name="w_bf", align_bytes=64)
         nc.scalar.copy(w_bf[:], w_raw[:].rearrange("p j m -> p m j"))
@@ -70,70 +74,104 @@ def tile_picked_ywmmse_wgt_p_kernel(tc, x_words, x_scales, w1, gain, hh, noise, 
         w_scales = keep.tile([P, M], U8, name="w_scales", align_bytes=64)
         nc.vector.quantize_mx(out=w_codes[:].bitcast(FP8X4), scales=w_scales[:], in_=w_bf[:].rearrange("p m j -> p (m j)"))
 
-
         def turn(dst, src, start, stop):
             nc.tensor.matmul(dst, lhsT=src, rhs=ident[:], is_transpose=True, start=start, stop=stop)
 
-        sums = []
-        for c, (c0, w) in enumerate(CHUNKS):
-            acc = psum.tile([P, w], F32, name="acc%d" % c)
-            for b in range(w // BLK):
-                turn(acc[:, b * BLK : (b + 1) * BLK], noise_t[:, 0:1].to_broadcast([P, BLK]), b == 0, False)
-            sums.append(acc)
+        def spread(col):
+            return col.to_broadcast([P, BLK])
 
         xs = []
         for h in range(2):
             t = keep.tile([P, HALF], U8, name="xs%d" % h, align_bytes=64)
             nc.vector.tensor_copy(t[:], scales[:].indirect(offs_t[:, h * 16 : (h + 1) * 16]))
             xs.append(t)
+        banks = []
         pp = keep.tile([P, S], F32, name="pp")
         for h in range(2):
             xw = keep.tile([P, HALF], U32, name="xw%d" % h, align_bytes=64)
             nc.vector.tensor_copy(xw[:], words[:].bitcast(U32).indirect(offs_t[:, h * 16 : (h + 1) * 16]))
             bank = psum.tile([P, S], F32, name="y%d" % h, tag="y%d" % h)
             y = bank[:, :HALF]
+            banks.append(bank)
             nc.tensor.matmul_mx(out=y, lhsT=w_codes[:].bitcast(FP8X4), lhsT_scale=w_scales[:],
                                 rhs=xw[:].bitcast(FP8X4), rhs_scale=xs[h][:], start=True, stop=True)
             nc.scalar.activation(pp[:, h * HALF : (h + 1) * HALF], y, ACT.Sigmoid)
-        nc.tensor.transpose(bank[:, HALF : HALF + BLK], rows[:], ident[:])
+        nc.tensor.transpose(banks[0][:, HALF : HALF + BLK], rows[:], ident[:])
         cols_t = keep.tile([P, 8], F32, name="cols_t")
-        nc.scalar.copy(cols_t[:], bank[:, HALF : HALF + 8])
-        nc.scalar.activation(warm_o[:, 1:2], pp[:, S - 1 : S], ACT.Abs_reciprocal_sqrt)
+        nc.scalar.copy(cols_t[:], banks[0][:, HALF : HALF + 8])
+        nc.scalar.activation(warm_o[:, 1:2], cols_t[:, 0:1], ACT.Abs_reciprocal_sqrt, scale=0.0, bias=1.0)
+        hh2 = keep.tile([P, 4], F32, name="hh2")
+        nc.gpsimd.tensor_tensor(hh2[:], cols_t[:, 0:4], cols_t[:, 0:4], ALU.mult)
+        own = keep.tile([P, 4], F32, name="own")
+        nc.gpsimd.tensor_tensor(own[:], hh2[:], cols_t[:, 4:8], ALU.mult)
 
-        pp_T = psum.tile([P, S], F32, name="pp_T", tag="turn")
-        for b in range(S // BLK):
+        pp_T = psum.tile([P, LAST], F32, name="pp_T")
+        for b in range(LAST // BLK):
             nc.tensor.transpose(pp_T[:, b * BLK : (b + 1) * BLK], pp[:, b * BLK : (b + 1) * BLK], ident[:])
+
+        def heard(c0, w, d):
+            t = keep.tile([P, w], F32, name="t%d_%d" % (c0, d))
+            nc.vector.tensor_tensor(t[:], pp[:].indirect(pos_t[d][:, c0 // 16 : (c0 + w) // 16]), gains[c0 // HALF][:, d, c0 % HALF : c0 % HALF + w], ALU.mult)
+            return t
+
+        def inverse(src, w, name, bias):
+            s = keep.tile([P, w], F32, name="s" + name, tag="s" + name)
+            nc.scalar.activation(s[:], src, ACT.Abs_reciprocal_sqrt, bias=bias)
+            r = keep.tile([P, w], F32, name="r" + name)
+            nc.scalar.activation(r[:], s[:], ACT.Square)
+            return r
+
+        rs = []
+        for c, (c0, w) in enumerate(TURNED):
+            nb = w // BLK
+            acc = psum.tile([P, w], F32, name="acc%d" % c)
+            for d in range(D):
+                t = heard(c0, w, d)
+                for b in range(nb):
+                    turn(acc[:, b * BLK : (b + 1) * BLK], t[:, b * BLK : (b + 1) * BLK], d == 0 and b == 0, d == D - 1 and b == nb - 1)
+                if d == 0:
+                    for b in range(nb):
+                        turn(acc[:, b * BLK : (b + 1) * BLK], spread(noise_t[:, 0:1]), False, False)
+            rs.append(inverse(acc[:], w, "%d" % c, 0.0))
+        t0 = heard(LAST, BLK, 0)
+        t1 = heard(LAST, BLK, 1)
+        t2 = heard(LAST, BLK, 2)
+        t01 = keep.tile([P, BLK], F32, name="t01")
+        nc.vector.tensor_tensor(t01[:], t0[:], t1[:], ALU.add)
+        t012 = keep.tile([P, BLK], F32, name="t012")
+        nc.vector.tensor_tensor(t012[:], t01[:], t2[:], ALU.add)
+        r_last = inverse(t012[:], BLK, "last", noise_t[:, 0:1])
+
+        late = keep.tile([P, S], F32, name="late", tag="gain1")
+        wide = psum.tile([P, 2, BLK], F32, name="wide")
+        nc.tensor.transpose(wide[:, 0, :], spread(own[:, 3:4]), ident[:])
+        nc.tensor.transpose(wide[:, 1, :], spread(cols_t[:, 7:8]), ident[:])
         res = []
-        for c, (c0, w) in enumerate(CHUNKS):
+        for c, (c0, w) in enumerate(TURNED):
             acc = psum.tile([P, w], F32, name="res%d" % c, tag="y0" if c == 0 else "res%d" % c)
             for b in range(w // BLK):
                 g = c0 // BLK + b
-                turn(acc[:, b * BLK : (b + 1) * BLK], cols_t[:, 4 + g : 5 + g].to_broadcast([P, BLK]), b == 0, False)
+                turn(acc[:, b * BLK : (b + 1) * BLK], spread(cols_t[:, 4 + g : 5 + g]), b == 0, False)
             res.append(acc)
 
-        rs = []
-        for c, (c0, w) in enumerate(CHUNKS):
+        for c, (c0, w) in enumerate(TURNED):
             nb = w // BLK
-            for d in range(D):
-                t = keep.tile([P, w], F32, name="t%d_%d" % (c, d))
-                nc.vector.tensor_tensor(t[:], pp[:].indirect(pos_t[d][:, c0 // 16 : (c0 + w) // 16]), gains[c0 // HALF][:, d, c0 % HALF : c0 % HALF + w], ALU.mult)
-                for b in range(nb):
-                    turn(sums[c][:, b * BLK : (b + 1) * BLK], t[:, b * BLK : (b + 1) * BLK], False, d == D - 1 and b == nb - 1)
-            s = keep.tile([P, w], F32, name="s%d" % c)
-            nc.scalar.activation(s[:], sums[c][:], ACT.Abs_reciprocal_sqrt)
-            r = keep.tile([P, w], F32, name="r%d" % c)
-            for b in range(nb):
-                g = c0 // BLK + b
-                nc.scalar.activation(r[:, b * BLK : (b + 1) * BLK], s[:, b * BLK : (b + 1) * BLK], ACT.Square, scale=cols_t[:, g : g + 1])
-            rs.append(r)
-        for c, (c0, w) in enumerate(CHUNKS):
-            nb = w // BLK
-            x = keep.tile([P, w], F32, name="x%d" % c)
+            x = late[:, c0 : c0 + w]
             for b in range(nb):
                 g = c0 // BLK + b
                 blk = slice(b * BLK, (b + 1) * BLK)
-                nc.vector.scalar_tensor_tensor(x[:, blk], rs[c][:, blk], cols_t[:, 4 + g : 5 + g], pp_T[:, g * BLK : (g + 1) * BLK], ALU.mult, ALU.mult)
+                nc.vector.scalar_tensor_tensor(x[:, blk], rs[c][:, blk], own[:, g : g + 1], pp_T[:, g * BLK : (g + 1) * BLK], ALU.mult, ALU.mult)
                 turn(res[c][:, blk], x[:, blk], False, b == nb - 1)
-            o = keep.tile([P, w], F32, name="o%d" % c)
-            nc.vector.tensor_copy(o[:], res[c][:])
-            nc.sync.dma_start(out[:, c0 : c0 + w], o[:])
+            o = keep.tile([P, w], F32, name="o%d" % c, tag="o0" if c == 0 else "slast")[:]
+            if c == 0:
+                nc.vector.tensor_copy(o, res[c][:])
+            else:
+                nc.scalar.copy(o, res[c][:])
+            nc.sync.dma_start(out[:, c0 : c0 + w], o)
+        q = late[:, LAST:]
+        nc.vector.tensor_tensor(q, pp[:, LAST:], wide[:, 0, :], ALU.mult)
+        x = keep.tile([P, BLK], F32, name="x_last")
+        nc.vector.tensor_tensor(x[:], r_last[:], q, ALU.mult)
+        o = keep.tile([P, BLK], F32, name="o_last")
+        nc.vector.tensor_tensor(o[:], x[:], wide[:, 1, :], ALU.add)
+        nc.sync.dma_start(out[:, LAST:], o[:])

@@ -99,11 +99,9 @@ def tile_picked_ywmmse_wgt_p_kernel(tc, x_words, x_scales, w1, gain, hh, noise, 
         nc.tensor.transpose(banks[0][:, HALF : HALF + BLK], rows[:], ident[:])
         cols_t = keep.tile([P, 8], F32, name="cols_t")
         nc.scalar.copy(cols_t[:], banks[0][:, HALF : HALF + 8])
-        nc.scalar.activation(warm_o[:, 1:2], cols_t[:, 0:1], ACT.Abs_reciprocal_sqrt, scale=0.0, bias=1.0)
-        hh2 = keep.tile([P, 4], F32, name="hh2")
-        nc.gpsimd.tensor_tensor(hh2[:], cols_t[:, 0:4], cols_t[:, 0:4], ALU.mult)
-        own = keep.tile([P, 4], F32, name="own")
-        nc.gpsimd.tensor_tensor(own[:], hh2[:], cols_t[:, 4:8], ALU.mult)
+        hh2 = keep.tile([P, 1], F32, name="hh2")
+        nc.scalar.activation(hh2[:], banks[0][:, HALF + 3 : HALF + 4], ACT.Square)
+        nc.scalar.activation(warm_o[:, 1:2], hh2[:], ACT.Abs_reciprocal_sqrt, scale=0.0, bias=1.0)
 
         pp_T = psum.tile([P, LAST], F32, name="pp_T")
         for b in range(LAST // BLK):
@@ -114,11 +112,12 @@ def tile_picked_ywmmse_wgt_p_kernel(tc, x_words, x_scales, w1, gain, hh, noise, 
             nc.vector.tensor_tensor(t[:], pp[:].indirect(pos_t[d][:, c0 // 16 : (c0 + w) // 16]), gains[c0 // HALF][:, d, c0 % HALF : c0 % HALF + w], ALU.mult)
             return t
 
-        def inverse(src, w, name, bias):
+        def inverse(src, w, name, bias, factors):
             s = keep.tile([P, w], F32, name="s" + name, tag="s" + name)
             nc.scalar.activation(s[:], src, ACT.Abs_reciprocal_sqrt, bias=bias)
             r = keep.tile([P, w], F32, name="r" + name)
-            nc.scalar.activation(r[:], s[:], ACT.Square)
+            for b, factor in enumerate(factors):
+                nc.scalar.activation(r[:, b * BLK : (b + 1) * BLK], s[:, b * BLK : (b + 1) * BLK], ACT.Square, scale=factor)
             return r
 
         rs = []
@@ -132,7 +131,7 @@ def tile_picked_ywmmse_wgt_p_kernel(tc, x_words, x_scales, w1, gain, hh, noise, 
                 if d == 0:
                     for b in range(nb):
                         turn(acc[:, b * BLK : (b + 1) * BLK], spread(noise_t[:, 0:1]), False, False)
-            rs.append(inverse(acc[:], w, "%d" % c, 0.0))
+            rs.append(inverse(acc[:], w, "%d" % c, 0.0, [cols_t[:, g : g + 1] for g in range(c0 // BLK, c0 // BLK + nb)]))
         t0 = heard(LAST, BLK, 0)
         t1 = heard(LAST, BLK, 1)
         t2 = heard(LAST, BLK, 2)
@@ -140,11 +139,11 @@ def tile_picked_ywmmse_wgt_p_kernel(tc, x_words, x_scales, w1, gain, hh, noise, 
         nc.vector.tensor_tensor(t01[:], t0[:], t1[:], ALU.add)
         t012 = keep.tile([P, BLK], F32, name="t012")
         nc.vector.tensor_tensor(t012[:], t01[:], t2[:], ALU.add)
-        r_last = inverse(t012[:], BLK, "last", noise_t[:, 0:1])
+        r_last = inverse(t012[:], BLK, "last", noise_t[:, 0:1], [1.0])
 
         late = keep.tile([P, S], F32, name="late", tag="gain1")
         wide = psum.tile([P, 2, BLK], F32, name="wide")
-        nc.tensor.transpose(wide[:, 0, :], spread(own[:, 3:4]), ident[:])
+        nc.tensor.transpose(wide[:, 0, :], spread(hh2[:, 0:1]), ident[:])
         nc.tensor.transpose(wide[:, 1, :], spread(cols_t[:, 7:8]), ident[:])
         res = []
         for c, (c0, w) in enumerate(TURNED):
@@ -160,7 +159,7 @@ def tile_picked_ywmmse_wgt_p_kernel(tc, x_words, x_scales, w1, gain, hh, noise, 
             for b in range(nb):
                 g = c0 // BLK + b
                 blk = slice(b * BLK, (b + 1) * BLK)
-                nc.vector.scalar_tensor_tensor(x[:, blk], rs[c][:, blk], own[:, g : g + 1], pp_T[:, g * BLK : (g + 1) * BLK], ALU.mult, ALU.mult)
+                nc.vector.scalar_tensor_tensor(x[:, blk], rs[c][:, blk], cols_t[:, 4 + g : 5 + g], pp_T[:, g * BLK : (g + 1) * BLK], ALU.mult, ALU.mult)
                 turn(res[c][:, blk], x[:, blk], False, b == nb - 1)
             o = keep.tile([P, w], F32, name="o%d" % c, tag="o0" if c == 0 else "slast")[:]
             if c == 0:
@@ -173,5 +172,5 @@ def tile_picked_ywmmse_wgt_p_kernel(tc, x_words, x_scales, w1, gain, hh, noise, 
         x = keep.tile([P, BLK], F32, name="x_last")
         nc.vector.tensor_tensor(x[:], r_last[:], q, ALU.mult)
         o = keep.tile([P, BLK], F32, name="o_last")
-        nc.vector.tensor_tensor(o[:], x[:], wide[:, 1, :], ALU.add)
+        nc.vector.scalar_tensor_tensor(o[:], x[:], 1.0, wide[:, 1, :], ALU.add, ALU.mult)
         nc.sync.dma_start(out[:, LAST:], o[:])

from contextlib import ExitStack

import concourse.mybir as mybir
from concourse.masks import make_identity

K, T, S, M, D = 512, 2048, 512, 128, 3
P = 128
PACK = 4
FLOPS = 2 * K * M * S

F32 = mybir.dt.float32
BF16 = mybir.dt.bfloat16
I32 = mybir.dt.int32
U32 = mybir.dt.uint32
U16 = mybir.dt.uint16
U8 = mybir.dt.uint8
FP8X4 = mybir.dt.float8_e4m3fn_x4
ALU = mybir.AluOpType
ACT = mybir.ActivationFunctionType

HALF = S // 2
BLK = 128
TURNED = ((0, 256), (256, 128))
LAST = S - BLK
EARLY = 512


def tile_picked_ywmmse_wgt_p_kernel(tc, x_words, x_scales, w1, gain, hh, noise, pri, offs, pos1, pos2, pos3, out):
    nc = tc.nc
    with ExitStack() as ctx:
        keep = ctx.enter_context(tc.tile_pool(name="keep", bufs=1))
        psum = ctx.enter_context(tc.psum_pool(name="psum", bufs=1))

        scales = keep.tile([P, T], U8, name="scales")
        nc.vector.memset(scales[:, : T // 2].bitcast(I32), 0)
        nc.gpsimd.memset(scales[:, T // 2 :].bitcast(I32), 0)
        warm = keep.tile([P, 2], F32, name="warm")
        nc.vector.memset(warm[:, 0:1], 0.0)
        warm_o = keep.tile([P, 2], F32, name="warm_o")
        nc.scalar.activation(warm_o[:, 0:1], warm[:, 0:1], ACT.Sigmoid)

        pos_t = [keep.tile([P, S // 16], U16, name="pos_t%d" % d) for d in range(D)]
        w_raw = keep.tile([P, PACK, M], F32, name="w_raw")
        nc.sync.dma_start(w_raw[:], w1.rearrange("(p j) m -> p j m", j=PACK))
        words = keep.tile([P, T], I32, name="words")
        words_hbm = x_words[0].rearrange("p n t -> p (n t)").bitcast(I32)
        nc.sync.dma_start(words[:, :EARLY], words_hbm[:, :EARLY])
        offs_t = keep.tile([P, S // 16], U16, name="offs_t")
        nc.sync.dma_start(offs_t[:], offs)
        for q in range(4):
            nc.sync.dma_start(scales[32 * q : 32 * q + 4, :].bitcast(I32), x_scales[0, 4 * q : 4 * q + 4, :].bitcast(I32))
        nc.sync.dma_start(words[:, EARLY:], words_hbm[:, EARLY:])

        rows = keep.tile([P, BLK], F32, name="rows")
        nc.gpsimd.memset(rows[:], 0.0)
        ident = keep.tile([P, P], F32, name="ident")
        make_identity(nc, ident[:])
        nc.sync.dma_start(rows[0:4, :], hh[0, :].rearrange("(b i) -> b i", i=BLK))
        nc.sync.dma_start(rows[4:8, :], pri[0, :].rearrange("(b i) -> b i", i=BLK))
        for t, pos in zip(pos_t, (pos1, pos2, pos3)):
            nc.sync.dma_start(t[:], pos)
        noise_t = keep.tile([P, 1], F32, name="noise_t")
        gains = []
        for h in range(2):
            t = keep.tile([P, D, HALF], F32, name="gain%d" % h, tag="gain%d" % h)
            nc.sync.dma_start(t[:], gain[:, :, h * HALF : (h + 1) * HALF].rearrange("d p s -> p d s"))
            gains.append(t)
            if h == 0:
                nc.sync.dma_start(noise_t[:], noise)

        w_bf = keep.tile([P, M, PACK], BF16, name="w_bf", align_bytes=64)
        nc.scalar.copy(w_bf[:], w_raw[:].rearrange("p j m -> p m j"))
        w_codes = keep.tile([P, M], U32, name="w_codes", align_bytes=64)
        w_scales = keep.tile([P, M], U8, name="w_scales", align_bytes=64)
        nc.vector.quantize_mx(out=w_codes[:].bitcast(FP8X4), scales=w_scales[:], in_=w_bf[:].rearrange("p m j -> p (m j)"))

        def turn(dst, src, start, stop):
            nc.tensor.matmul(dst, lhsT=src, rhs=ident[:], is_transpose=True, start=start, stop=stop)

        def spread(col):
            return col.to_broadcast([P, BLK])

        xs = []
        for h in range(2):
            t = keep.tile([P, HALF], U8, name="xs%d" % h, align_bytes=64)
            nc.vector.tensor_copy(t[:], scales[:].indirect(offs_t[:, h * 16 : (h + 1) * 16]))
            xs.append(t)
        banks = []
        pp = keep.tile([P, S], F32, name="pp")
        for h in range(2):
            xw = keep.tile([P, HALF], U32, name="xw%d" % h, align_bytes=64)
            nc.vector.tensor_copy(xw[:], words[:].bitcast(U32).indirect(offs_t[:, h * 16 : (h + 1) * 16]))
            bank = psum.tile([P, S], F32, name="y%d" % h, tag="y%d" % h)
            y = bank[:, :HALF]
            banks.append(bank)
            nc.tensor.matmul_mx(out=y, lhsT=w_codes[:].bitcast(FP8X4), lhsT_scale=w_scales[:],
                                rhs=xw[:].bitcast(FP8X4), rhs_scale=xs[h][:], start=True, stop=True)
            nc.scalar.activation(pp[:, h * HALF : (h + 1) * HALF], y, ACT.Sigmoid)
        nc.tensor.transpose(banks[0][:, HALF : HALF + BLK], rows[:], ident[:])
        cols_t = keep.tile([P, 8], F32, name="cols_t")
        nc.scalar.copy(cols_t[:], banks[0][:, HALF : HALF + 8])
        hh2 = keep.tile([P, 1], F32, name="hh2")
        nc.scalar.activation(hh2[:], banks[0][:, HALF + 3 : HALF + 4], ACT.Square)
        nc.scalar.activation(warm_o[:, 1:2], hh2[:], ACT.Abs_reciprocal_sqrt, scale=0.0, bias=1.0)

        pp_T = psum.tile([P, LAST], F32, name="pp_T")
        for b in range(LAST // BLK):
            nc.tensor.transpose(pp_T[:, b * BLK : (b + 1) * BLK], pp[:, b * BLK : (b + 1) * BLK], ident[:])

        def heard(c0, w, d):
            t = keep.tile([P, w], F32, name="t%d_%d" % (c0, d))
            nc.vector.tensor_tensor(t[:], pp[:].indirect(pos_t[d][:, c0 // 16 : (c0 + w) // 16]), gains[c0 // HALF][:, d, c0 % HALF : c0 % HALF + w], ALU.mult)
            return t

        def inverse(src, w, name, bias, factors):
            s = keep.tile([P, w], F32, name="s" + name, tag="s" + name)
            nc.scalar.activation(s[:], src, ACT.Abs_reciprocal_sqrt, bias=bias)
            r = keep.tile([P, w], F32, name="r" + name)
            for b, factor in enumerate(factors):
                nc.scalar.activation(r[:, b * BLK : (b + 1) * BLK], s[:, b * BLK : (b + 1) * BLK], ACT.Square, scale=factor)
            return r

        rs = []
        for c, (c0, w) in enumerate(TURNED):
            nb = w // BLK
            acc = psum.tile([P, w], F32, name="acc%d" % c)
            for d in range(D):
                t = heard(c0, w, d)
                for b in range(nb):
                    turn(acc[:, b * BLK : (b + 1) * BLK], t[:, b * BLK : (b + 1) * BLK], d == 0 and b == 0, d == D - 1 and b == nb - 1)
                if d == 0:
                    for b in range(nb):
                        turn(acc[:, b * BLK : (b + 1) * BLK], spread(noise_t[:, 0:1]), False, False)
            rs.append(inverse(acc[:], w, "%d" % c, 0.0, [cols_t[:, g : g + 1] for g in range(c0 // BLK, c0 // BLK + nb)]))
        t0 = heard(LAST, BLK, 0)
        t1 = heard(LAST, BLK, 1)
        t2 = heard(LAST, BLK, 2)
        t01 = keep.tile([P, BLK], F32, name="t01")
        nc.vector.tensor_tensor(t01[:], t0[:], t1[:], ALU.add)
        t012 = keep.tile([P, BLK], F32, name="t012")
        nc.vector.tensor_tensor(t012[:], t01[:], t2[:], ALU.add)
        r_last = inverse(t012[:], BLK, "last", noise_t[:, 0:1], [1.0])

        late = keep.tile([P, S], F32, name="late", tag="gain1")
        wide = psum.tile([P, 2, BLK], F32, name="wide")
        nc.tensor.transpose(wide[:, 0, :], spread(hh2[:, 0:1]), ident[:])
        nc.tensor.transpose(wide[:, 1, :], spread(cols_t[:, 7:8]), ident[:])
        res = []
        for c, (c0, w) in enumerate(TURNED):
            acc = psum.tile([P, w], F32, name="res%d" % c, tag="y0" if c == 0 else "res%d" % c)
            for b in range(w // BLK):
                g = c0 // BLK + b
                turn(acc[:, b * BLK : (b + 1) * BLK], spread(cols_t[:, 4 + g : 5 + g]), b == 0, False)
            res.append(acc)

        for c, (c0, w) in enumerate(TURNED):
            nb = w // BLK
            x = late[:, c0 : c0 + w]
            for b in range(nb):
                g = c0 // BLK + b
                blk = slice(b * BLK, (b + 1) * BLK)
                nc.vector.scalar_tensor_tensor(x[:, blk], rs[c][:, blk], cols_t[:, 4 + g : 5 + g], pp_T[:, g * BLK : (g + 1) * BLK], ALU.mult, ALU.mult)
                turn(res[c][:, blk], x[:, blk], False, b == nb - 1)
            o = keep.tile([P, w], F32, name="o%d" % c, tag="o0" if c == 0 else "slast")[:]
            if c == 0:
                nc.vector.tensor_copy(o, res[c][:])
            else:
                nc.scalar.copy(o, res[c][:])
            nc.sync.dma_start(out[:, c0 : c0 + w], o)
        q = late[:, LAST:]
        nc.vector.tensor_tensor(q, pp[:, LAST:], wide[:, 0, :], ALU.mult)
        x = keep.tile([P, BLK], F32, name="x_last")
        nc.vector.tensor_tensor(x[:], r_last[:], q, ALU.mult)
        o = keep.tile([P, BLK], F32, name="o_last")
        nc.vector.scalar_tensor_tensor(o[:], x[:], 1.0, wide[:, 1, :], ALU.add, ALU.mult)
        nc.sync.dma_start(out[:, LAST:], o[:])
